import numpy as np
import ml_dtypes


def mxq(x, axis, fmt="e4m3"):
    dtype, down = {"e4m3": (ml_dtypes.float8_e4m3fn, 7), "e5m2": (ml_dtypes.float8_e5m2, 14)}[fmt]
    v = np.moveaxis(np.asarray(x, np.float32).astype(ml_dtypes.bfloat16).astype(np.float64), axis, -1)
    blocks = v.reshape(v.shape[:-1] + (-1, 32))
    amax = np.abs(blocks).max(-1, keepdims=True)
    byte = np.maximum(np.where(amax > 0, np.frexp(amax)[1] - 1 + 127, 0) - down, 1)
    scale = np.exp2(byte - 127.0)
    codes = (blocks / scale).astype(np.float32).astype(dtype).astype(np.float64)
    return np.moveaxis((codes * scale).reshape(v.shape), -1, axis)


WIDE = False


def mx_kscale(k):
    if not WIDE:
        return np.ones(k)
    levels = np.array([10, -10, 5, -5, 0])
    if k % 512:
        return np.exp2(np.random.permutation(np.resize(levels, k // 32))).repeat(32)
    a = np.empty((k // 512, 16))
    for p in range(k // 512):
        a[p, :8] = np.random.permutation(np.resize(levels, 8))
        for g in range(8):
            far = levels[np.abs(levels - a[p, g]) >= 10]
            a[p, g + 8] = far[np.random.randint(len(far))]
    return np.exp2(a.ravel()).repeat(32)


def f64(x):
    return np.asarray(x).astype(np.float64)


def striped(idx):
    return np.tile(idx.reshape(-1, 16).T, (8, 1)).astype(np.uint16)


def unstriped(offs):
    return offs[:16].T.reshape(-1).astype(np.int64)


def pack_weight(w):
    k, n = w.shape
    w = f64(np.asarray(w, np.float32).astype(ml_dtypes.bfloat16)).reshape(k // 32, 32, n)
    amax = np.abs(w).max(1)
    byte = np.clip(np.where(amax > 0, np.frexp(amax)[1] - 1 + 127 - 7, 1), 1, 254)
    scaled = (w * np.exp2(127.0 - byte)[:, None, :]).reshape(k, n).astype(np.float32)
    words = np.ascontiguousarray(scaled.reshape(k // 512, 128, 4, n).transpose(0, 1, 3, 2)).astype(ml_dtypes.float8_e4m3fn).view(np.uint8)
    return words, np.ascontiguousarray(byte.astype(np.uint8).reshape(k // 512, 16, n))


def unpack_weight(words, scales):
    g, p, n, _ = words.shape
    vals = np.ascontiguousarray(words).view(ml_dtypes.float8_e4m3fn).astype(np.float64) * np.repeat(np.exp2(scales.astype(np.float64) - 127.0), 8, axis=1)[..., None]
    return vals.transpose(0, 1, 3, 2).reshape(g * 512, n)


K, T, S, N = 512, 2048, 512, 128
P = 2 ** 7


def setup_inputs():
    n = np.random.standard_normal
    s = mx_kscale(K)[:, None]
    packed_xT = pack_weight(n((K, T)) * s)
    return {
        "x_words": packed_xT[0],
        "x_scales": packed_xT[1],
        "w1": (n((K, N)) / np.sqrt(K) / s).astype(np.float32),
        "w2": (n((K, N)) / np.sqrt(K) / s).astype(np.float32),
        "w3": (n((K, N)) / np.sqrt(K) / s).astype(np.float32),
        "envl": (np.tile(np.random.uniform(0.0, 1.2, T), (P, 1))).astype(np.float32),
        "offs": striped(np.random.permutation(T)[:S]),
        "lag": striped(np.random.permutation(T)[:S]),
    }


def reference(x_words, x_scales, w1, w2, w3, envl, offs, lag):
    xq = unpack_weight(x_words, x_scales)[:, unstriped(offs)]
    y0 = mxq(f64(w1), 0, "e4m3").T @ xq
    y1 = mxq(f64(w2), 0, "e4m3").T @ xq
    x_lag = unpack_weight(x_words, x_scales)[:, unstriped(lag)]
    y2 = mxq(f64(w3), 0, "e4m3").T @ x_lag
    return y0 + y1 * ((f64(envl)[:1][:, unstriped(offs)]) ** 2) + y2 * (f64(envl)[:1][:, unstriped(lag)] + 0.5 * ((f64(envl)[:1][:, unstriped(offs)]) ** 2))

@@ -1,0 +1,151 @@
+from contextlib import ExitStack
+
+import concourse.mybir as mybir
+from concourse.masks import make_identity
+
+K, T, S, M = 512, 2048, 512, 128
+FLOPS = 3 * 2 * K * M * S
+BYTES = K * T + (K // 32) * T + 3 * K * M * 4 + T * 4 + 2 * 128 * (S // 16) * 2 + M * S * 4
+
+F32 = mybir.dt.float32
+BF16 = mybir.dt.bfloat16
+I32 = mybir.dt.int32
+U32 = mybir.dt.uint32
+U16 = mybir.dt.uint16
+U8 = mybir.dt.uint8
+FP8X4 = mybir.dt.float8_e4m3fn_x4
+ACT = mybir.ActivationFunctionType
+ALU = mybir.AluOpType
+
+P = 128
+PACK = 4
+HALF = S // 2
+BLOCKS = S // P
+ENV_ROW = P - 1
+
+
+def tile_picked_ymempol_lin_p_kernel(tc, x_words, x_scales, w1, w2, w3, envl, offs, lag, out):
+    nc = tc.nc
+    with ExitStack() as ctx:
+        sb = ctx.enter_context(tc.tile_pool(name="sb", bufs=1))
+        ps = ctx.enter_context(tc.psum_pool(name="ps", bufs=1))
+
+        offs_t = sb.tile([P, S // 16], U16, name="offs_t")
+        lag_t = sb.tile([P, S // 16], U16, name="lag_t")
+        words = sb.tile([P, T], I32, name="words")
+        scales = sb.tile([P, T], U8, name="scales", tag="shared", align_bytes=64)
+        env = sb.tile([P, T], F32, name="env")
+        w_raw = [sb.tile([P, PACK, M], F32, name=f"w_raw{i}") for i in range(3)]
+        ident = sb.tile([P, P], F32, name="ident")
+
+        nc.vector.memset(scales[:].bitcast(I32), 0)
+        nc.vector.memset(env[0:ENV_ROW, :], 0.0)
+        make_identity(nc, ident[:])
+
+        nc.sync.dma_start(offs_t[:], offs)
+        for q in range(4):
+            nc.sync.dma_start(scales[32 * q : 32 * q + 4, :].bitcast(I32), x_scales[0, 4 * q : 4 * q + 4, :].bitcast(I32))
+        nc.sync.dma_start(env[ENV_ROW:P, :], envl[0:1, :])
+        nc.sync.dma_start(lag_t[:], lag)
+        nc.sync.dma_start(words[:], x_words[0].rearrange("p n t -> p (n t)").bitcast(I32))
+        for raw, w in zip(w_raw, (w1, w2, w3)):
+            nc.sync.dma_start(raw[:], w.rearrange("(p j) m -> p j m", j=PACK))
+
+        def interleave(grouped, raw):
+            nc.scalar.activation(
+                grouped.rearrange("p (c i) j -> p c j i", i=4), raw[:].rearrange("p j (c i) -> p c j i", i=4), ACT.Copy
+            )
+
+        def quantize(grouped, width, name):
+            codes = sb.tile([P, width], U32, name=name + "_codes", align_bytes=64)
+            plane = sb.tile([P, width], U8, name=name + "_plane", align_bytes=64)
+            nc.vector.quantize_mx(out=codes[:].bitcast(FP8X4), scales=plane[:], in_=grouped[:].rearrange("p m j -> p (m j)"))
+            return codes, plane
+
+        def gather(window, offsets, width, dtype, name):
+            picked = sb.tile([P, width], dtype, name=name, align_bytes=64)
+            nc.vector.tensor_copy(picked[:], window.indirect(offsets))
+            return picked
+
+        def turn(picked_env, tag):
+            bank = ps.tile([P, BLOCKS, P], F32, name="turned_" + tag, tag=tag)
+            for b in range(BLOCKS):
+                nc.tensor.transpose(bank[:, b, :], picked_env[:, P * b : P * (b + 1)], ident[:])
+            return bank
+
+        w12_bf = sb.tile([P, 2 * M, PACK], BF16, name="w12_bf", align_bytes=64)
+        w3_bf = sb.tile([P, M, PACK], BF16, name="w3_bf", align_bytes=64)
+        interleave(w12_bf[:, 0:M, :], w_raw[0])
+        interleave(w12_bf[:, M : 2 * M, :], w_raw[1])
+        interleave(w3_bf[:], w_raw[2])
+
+        xo_s = gather(scales[:], offs_t[:], S, U8, "xo_s")
+        env_o = gather(env[:], offs_t[:], S, F32, "env_o")
+        env_l = gather(env[:], lag_t[:], S, F32, "env_l")
+
+        eo_bank = turn(env_o, "bank_a")
+        el_bank = turn(env_l, "bank_b")
+        sq = sb.tile([P, BLOCKS], F32, name="sq")
+        half_sq = sb.tile([P, BLOCKS], F32, name="half_sq")
+        cf = sb.tile([P, BLOCKS], F32, name="cf")
+        nc.scalar.activation(sq[:], eo_bank[:, :, ENV_ROW], ACT.Square)
+        nc.scalar.activation(half_sq[:], sq[:], ACT.Copy, scale=0.5)
+        for b in range(BLOCKS):
+            nc.scalar.activation(cf[:, b : b + 1], el_bank[:, b, ENV_ROW:P], ACT.Identity, bias=half_sq[:, b : b + 1])
+
+        w12_c, w12_s = quantize(w12_bf, 2 * M, "w12")
+        xo_w = gather(words[:].bitcast(U32), offs_t[:], S, U32, "xo_w")
+        xl_s = gather(scales[:], lag_t[:], S, U8, "xl_s")
+        w3_c, w3_s = quantize(w3_bf, M, "w3")
+        xl_w = sb.tile([P, S], U32, name="xl_w", tag="shared", align_bytes=64)
+        for h in range(2):
+            nc.vector.tensor_copy(
+                xl_w[:, HALF * h : HALF * (h + 1)], words[:].bitcast(U32).indirect(lag_t[:, h * (HALF // 16) : (h + 1) * (HALF // 16)])
+            )
+
+        y1_bank = ps.tile([P, BLOCKS, M], F32, name="y1_bank")
+        for b in range(BLOCKS):
+            cols = slice(P * b, P * (b + 1))
+            nc.tensor.matmul_mx(
+                out=y1_bank[:, b, :], lhsT=xo_w[:, cols].bitcast(FP8X4), lhsT_scale=xo_s[:, cols],
+                rhs=w12_c[:, M : 2 * M].bitcast(FP8X4), rhs_scale=w12_s[:, M : 2 * M], start=True, stop=True,
+            )
+        y0_bank = ps.tile([M, S], F32, name="y0_bank")
+        nc.tensor.matmul_mx(
+            out=y0_bank[:], lhsT=w12_c[:, 0:M].bitcast(FP8X4), lhsT_scale=w12_s[:, 0:M],
+            rhs=xo_w[:].bitcast(FP8X4), rhs_scale=xo_s[:], start=True, stop=True,
+        )
+        t1 = sb.tile([P, BLOCKS, M], F32, name="t1")
+        for b in range(BLOCKS):
+            nc.scalar.activation(t1[:, b, :], y1_bank[:, b, :], ACT.Copy, scale=sq[:, b : b + 1])
+        y0 = sb.tile([M, S], F32, name="y0")
+        nc.scalar.copy(y0[:], y0_bank[:])
+
+        sums = [ps.tile([M, HALF], F32, name=f"sums{h}") for h in range(2)]
+        for b in range(BLOCKS):
+            h, i = divmod(b, 2)
+            nc.tensor.matmul(sums[h][:, P * i : P * (i + 1)], t1[:, b, :], ident[:], start=(i == 0), stop=False, is_transpose=True)
+
+        y2_banks = [
+            ps.tile([P, M], F32, name=f"y2_bank{b}", tag=tag) for b, tag in enumerate(("bank_a", "bank_b", "bank_c", "bank_d"))
+        ]
+        t2 = [sb.tile([P, M], F32, name=f"t2_{b}") for b in range(BLOCKS)]
+        for h in range(2):
+            for i in range(2):
+                b = 2 * h + i
+                nc.tensor.matmul_mx(
+                    out=y2_banks[b][:], lhsT=xl_w[:, P * b : P * (b + 1)].bitcast(FP8X4), lhsT_scale=xl_s[:, P * b : P * (b + 1)],
+                    rhs=w3_c[:].bitcast(FP8X4), rhs_scale=w3_s[:], start=True, stop=True,
+                )
+            for i in range(2):
+                b = 2 * h + i
+                if b == BLOCKS - 1:
+                    nc.vector.tensor_scalar(t2[b][:], y2_banks[b][:], cf[:, b : b + 1], None, ALU.mult)
+                else:
+                    nc.scalar.activation(t2[b][:], y2_banks[b][:], ACT.Copy, scale=cf[:, b : b + 1])
+            for i in range(2):
+                nc.tensor.matmul(sums[h][:, P * i : P * (i + 1)], t2[2 * h + i][:], ident[:], start=False, stop=(i == 1), is_transpose=True)
+            cols = slice(HALF * h, HALF * (h + 1))
+            res = sb.tile([M, HALF], F32, name=f"res{h}")
+            nc.vector.tensor_tensor(res[:], sums[h][:], y0[:, cols], ALU.add)
+            nc.sync.dma_start(out[:, cols], res[:])

@@ -1,11 +1,9 @@
 from contextlib import ExitStack
 
 import concourse.mybir as mybir
-from concourse.masks import make_identity
 
 K, T, S, M = 512, 2048, 512, 128
 FLOPS = 3 * 2 * K * M * S
-BYTES = K * T + (K // 32) * T + 3 * K * M * 4 + T * 4 + 2 * 128 * (S // 16) * 2 + M * S * 4
 
 F32 = mybir.dt.float32
 BF16 = mybir.dt.bfloat16
@@ -20,8 +18,6 @@ ALU = mybir.AluOpType
 P = 128
 PACK = 4
 HALF = S // 2
-BLOCKS = S // P
-ENV_ROW = P - 1
 
 
 def tile_picked_ymempol_lin_p_kernel(tc, x_words, x_scales, w1, w2, w3, envl, offs, lag, out):
@@ -33,119 +29,77 @@ def tile_picked_ymempol_lin_p_kernel(tc, x_words, x_scales, w1, w2, w3, envl, of
         offs_t = sb.tile([P, S // 16], U16, name="offs_t")
         lag_t = sb.tile([P, S // 16], U16, name="lag_t")
         words = sb.tile([P, T], I32, name="words")
-        scales = sb.tile([P, T], U8, name="scales", tag="shared", align_bytes=64)
-        env = sb.tile([P, T], F32, name="env")
-        w_raw = [sb.tile([P, PACK, M], F32, name=f"w_raw{i}") for i in range(3)]
-        ident = sb.tile([P, P], F32, name="ident")
+        scales = sb.tile([P, T], U8, name="scales")
+        env = sb.tile([P, T], F32, name="env", tag="env")
+        w1_raw = sb.tile([P, PACK, M], F32, name="w1_raw")
+        w2_raw = sb.tile([P, PACK, M], F32, name="w2_raw")
+        w3_raw = sb.tile([P, PACK, M], F32, name="w3_raw")
 
         nc.vector.memset(scales[:].bitcast(I32), 0)
-        nc.vector.memset(env[0:ENV_ROW, :], 0.0)
-        make_identity(nc, ident[:])
 
-        nc.sync.dma_start(offs_t[:], offs)
+        nc.sync.dma_start(lag_t[:], lag)
         for q in range(4):
             nc.sync.dma_start(scales[32 * q : 32 * q + 4, :].bitcast(I32), x_scales[0, 4 * q : 4 * q + 4, :].bitcast(I32))
-        nc.sync.dma_start(env[ENV_ROW:P, :], envl[0:1, :])
-        nc.sync.dma_start(lag_t[:], lag)
+        nc.sync.dma_start(offs_t[:], offs)
         nc.sync.dma_start(words[:], x_words[0].rearrange("p n t -> p (n t)").bitcast(I32))
-        for raw, w in zip(w_raw, (w1, w2, w3)):
-            nc.sync.dma_start(raw[:], w.rearrange("(p j) m -> p j m", j=PACK))
+        nc.sync.dma_start(w3_raw[:], w3.rearrange("(p j) m -> p j m", j=PACK))
+        nc.sync.dma_start(w2_raw[:], w2.rearrange("(p j) m -> p j m", j=PACK))
+        nc.sync.dma_start(env[:], envl)
+        nc.sync.dma_start(w1_raw[:], w1.rearrange("(p j) m -> p j m", j=PACK))
 
-        def interleave(grouped, raw):
-            nc.scalar.activation(
-                grouped.rearrange("p (c i) j -> p c j i", i=4), raw[:].rearrange("p j (c i) -> p c j i", i=4), ACT.Copy
-            )
-
-        def quantize(grouped, width, name):
-            codes = sb.tile([P, width], U32, name=name + "_codes", align_bytes=64)
-            plane = sb.tile([P, width], U8, name=name + "_plane", align_bytes=64)
-            nc.vector.quantize_mx(out=codes[:].bitcast(FP8X4), scales=plane[:], in_=grouped[:].rearrange("p m j -> p (m j)"))
-            return codes, plane
-
-        def gather(window, offsets, width, dtype, name):
-            picked = sb.tile([P, width], dtype, name=name, align_bytes=64)
+        def gather(window, offsets, dtype, name, tag):
+            picked = sb.tile([P, S], dtype, name=name, tag=tag, align_bytes=64)
             nc.vector.tensor_copy(picked[:], window.indirect(offsets))
             return picked
 
-        def turn(picked_env, tag):
-            bank = ps.tile([P, BLOCKS, P], F32, name="turned_" + tag, tag=tag)
-            for b in range(BLOCKS):
-                nc.tensor.transpose(bank[:, b, :], picked_env[:, P * b : P * (b + 1)], ident[:])
+        def quantize(raw, name):
+            grouped = sb.tile([P, M, PACK], BF16, name=name + "_grouped", tag=name + "_grouped", align_bytes=64)
+            nc.scalar.activation(
+                grouped[:].rearrange("p (c i) j -> p c j i", i=4), raw[:].rearrange("p j (c i) -> p c j i", i=4), ACT.Copy
+            )
+            codes = sb.tile([P, M], U32, name=name + "_codes", align_bytes=64)
+            plane = sb.tile([P, M], U8, name=name + "_plane", align_bytes=64)
+            nc.vector.quantize_mx(out=codes[:].bitcast(FP8X4), scales=plane[:], in_=grouped[:].rearrange("p m j -> p (m j)"))
+            return codes, plane
+
+        def product(weights, x_codes, x_plane, name):
+            bank = ps.tile([M, S], F32, name=name)
+            nc.tensor.matmul_mx(
+                out=bank[:], lhsT=weights[0][:].bitcast(FP8X4), lhsT_scale=weights[1][:],
+                rhs=x_codes[:].bitcast(FP8X4), rhs_scale=x_plane[:], start=True, stop=True,
+            )
             return bank
 
-        w12_bf = sb.tile([P, 2 * M, PACK], BF16, name="w12_bf", align_bytes=64)
-        w3_bf = sb.tile([P, M, PACK], BF16, name="w3_bf", align_bytes=64)
-        interleave(w12_bf[:, 0:M, :], w_raw[0])
-        interleave(w12_bf[:, M : 2 * M, :], w_raw[1])
-        interleave(w3_bf[:], w_raw[2])
+        xl_plane = gather(scales[:], lag_t[:], U8, "xl_plane", "xl_plane")
+        xo_plane = gather(scales[:], offs_t[:], U8, "xo_plane", "xo_plane")
+        xl_codes = gather(words[:].bitcast(U32), lag_t[:], U32, "xl_codes", "xl_codes")
+        w3_q = quantize(w3_raw, "w3")
+        w2_q = quantize(w2_raw, "w2")
+        xo_codes = gather(words[:].bitcast(U32), offs_t[:], U32, "xo_codes", "w2_grouped")
 
-        xo_s = gather(scales[:], offs_t[:], S, U8, "xo_s")
-        env_o = gather(env[:], offs_t[:], S, F32, "env_o")
-        env_l = gather(env[:], lag_t[:], S, F32, "env_l")
+        y2_bank = product(w3_q, xl_codes, xl_plane, "y2_bank")
+        y1_bank = product(w2_q, xo_codes, xo_plane, "y1_bank")
+        y2 = sb.tile([M, S], F32, name="y2")
+        nc.scalar.copy(y2[:], y2_bank[:])
 
-        eo_bank = turn(env_o, "bank_a")
-        el_bank = turn(env_l, "bank_b")
-        sq = sb.tile([P, BLOCKS], F32, name="sq")
-        half_sq = sb.tile([P, BLOCKS], F32, name="half_sq")
-        cf = sb.tile([P, BLOCKS], F32, name="cf")
-        nc.scalar.activation(sq[:], eo_bank[:, :, ENV_ROW], ACT.Square)
-        nc.scalar.activation(half_sq[:], sq[:], ACT.Copy, scale=0.5)
-        for b in range(BLOCKS):
-            nc.scalar.activation(cf[:, b : b + 1], el_bank[:, b, ENV_ROW:P], ACT.Identity, bias=half_sq[:, b : b + 1])
+        env_o = gather(env[:], offs_t[:], F32, "env_o", "env_o")
+        lag_term = sb.tile([M, S], F32, name="lag_term")
+        nc.vector.tensor_tensor(lag_term[:], env[:].indirect(lag_t[:]), y2[:], ALU.mult)
+        power = sb.tile([P, S], F32, name="power")
+        nc.scalar.activation(power[:], env_o[:], ACT.Square)
+        mixed = sb.tile([M, S], F32, name="mixed", tag="env")
+        nc.vector.scalar_tensor_tensor(mixed[:], y2[:], 0.5, y1_bank[:], ALU.mult, ALU.add)
 
-        w12_c, w12_s = quantize(w12_bf, 2 * M, "w12")
-        xo_w = gather(words[:].bitcast(U32), offs_t[:], S, U32, "xo_w")
-        xl_s = gather(scales[:], lag_t[:], S, U8, "xl_s")
-        w3_c, w3_s = quantize(w3_bf, M, "w3")
-        xl_w = sb.tile([P, S], U32, name="xl_w", tag="shared", align_bytes=64)
-        for h in range(2):
-            nc.vector.tensor_copy(
-                xl_w[:, HALF * h : HALF * (h + 1)], words[:].bitcast(U32).indirect(lag_t[:, h * (HALF // 16) : (h + 1) * (HALF // 16)])
-            )
+        w1_q = quantize(w1_raw, "w1")
+        y0_bank = product(w1_q, xo_codes, xo_plane, "y0_bank")
+        power_term = sb.tile([M, S], F32, name="power_term", tag="w1_grouped", align_bytes=64)
+        nc.vector.tensor_tensor(power_term[:], power[:], mixed[:], ALU.mult)
 
-        y1_bank = ps.tile([P, BLOCKS, M], F32, name="y1_bank")
-        for b in range(BLOCKS):
-            cols = slice(P * b, P * (b + 1))
-            nc.tensor.matmul_mx(
-                out=y1_bank[:, b, :], lhsT=xo_w[:, cols].bitcast(FP8X4), lhsT_scale=xo_s[:, cols],
-                rhs=w12_c[:, M : 2 * M].bitcast(FP8X4), rhs_scale=w12_s[:, M : 2 * M], start=True, stop=True,
-            )
-        y0_bank = ps.tile([M, S], F32, name="y0_bank")
-        nc.tensor.matmul_mx(
-            out=y0_bank[:], lhsT=w12_c[:, 0:M].bitcast(FP8X4), lhsT_scale=w12_s[:, 0:M],
-            rhs=xo_w[:].bitcast(FP8X4), rhs_scale=xo_s[:], start=True, stop=True,
-        )
-        t1 = sb.tile([P, BLOCKS, M], F32, name="t1")
-        for b in range(BLOCKS):
-            nc.scalar.activation(t1[:, b, :], y1_bank[:, b, :], ACT.Copy, scale=sq[:, b : b + 1])
-        y0 = sb.tile([M, S], F32, name="y0")
-        nc.scalar.copy(y0[:], y0_bank[:])
-
-        sums = [ps.tile([M, HALF], F32, name=f"sums{h}") for h in range(2)]
-        for b in range(BLOCKS):
-            h, i = divmod(b, 2)
-            nc.tensor.matmul(sums[h][:, P * i : P * (i + 1)], t1[:, b, :], ident[:], start=(i == 0), stop=False, is_transpose=True)
-
-        y2_banks = [
-            ps.tile([P, M], F32, name=f"y2_bank{b}", tag=tag) for b, tag in enumerate(("bank_a", "bank_b", "bank_c", "bank_d"))
-        ]
-        t2 = [sb.tile([P, M], F32, name=f"t2_{b}") for b in range(BLOCKS)]
-        for h in range(2):
-            for i in range(2):
-                b = 2 * h + i
-                nc.tensor.matmul_mx(
-                    out=y2_banks[b][:], lhsT=xl_w[:, P * b : P * (b + 1)].bitcast(FP8X4), lhsT_scale=xl_s[:, P * b : P * (b + 1)],
-                    rhs=w3_c[:].bitcast(FP8X4), rhs_scale=w3_s[:], start=True, stop=True,
-                )
-            for i in range(2):
-                b = 2 * h + i
-                if b == BLOCKS - 1:
-                    nc.vector.tensor_scalar(t2[b][:], y2_banks[b][:], cf[:, b : b + 1], None, ALU.mult)
-                else:
-                    nc.scalar.activation(t2[b][:], y2_banks[b][:], ACT.Copy, scale=cf[:, b : b + 1])
-            for i in range(2):
-                nc.tensor.matmul(sums[h][:, P * i : P * (i + 1)], t2[2 * h + i][:], ident[:], start=False, stop=(i == 1), is_transpose=True)
-            cols = slice(HALF * h, HALF * (h + 1))
-            res = sb.tile([M, HALF], F32, name=f"res{h}")
-            nc.vector.tensor_tensor(res[:], sums[h][:], y0[:, cols], ALU.add)
-            nc.sync.dma_start(out[:, cols], res[:])
+        halves = [slice(HALF * h, HALF * (h + 1)) for h in range(2)]
+        both = sb.tile([M, S], F32, name="both")
+        res = sb.tile([M, S], F32, name="res")
+        for cols in halves:
+            nc.vector.tensor_tensor(both[:, cols], power_term[:, cols], lag_term[:, cols], ALU.add)
+        for cols in halves:
+            nc.vector.tensor_tensor(res[:, cols], y0_bank[:, cols], both[:, cols], ALU.add)
+            nc.sync.dma_start(out[:, cols], res[:, cols])

@@ -4,6 +4,7 @@ import concourse.mybir as mybir
 
 K, T, S, M = 512, 2048, 512, 128
 FLOPS = 3 * 2 * K * M * S
+BYTES = K * T + (K // 32) * T + 3 * K * M * 4 + T * 4 + 2 * 128 * (S // 16) * 2 + M * S * 4
 
 F32 = mybir.dt.float32
 BF16 = mybir.dt.bfloat16
@@ -18,6 +19,8 @@ ALU = mybir.AluOpType
 P = 128
 PACK = 4
 HALF = S // 2
+BLOCKS = S // P
+ENV_ROW = P - 1
 
 
 def tile_picked_ymempol_lin_p_kernel(tc, x_words, x_scales, w1, w2, w3, envl, offs, lag, out):
@@ -30,76 +33,115 @@ def tile_picked_ymempol_lin_p_kernel(tc, x_words, x_scales, w1, w2, w3, envl, of
         lag_t = sb.tile([P, S // 16], U16, name="lag_t")
         words = sb.tile([P, T], I32, name="words")
         scales = sb.tile([P, T], U8, name="scales")
-        env = sb.tile([P, T], F32, name="env", tag="env")
-        w1_raw = sb.tile([P, PACK, M], F32, name="w1_raw")
-        w2_raw = sb.tile([P, PACK, M], F32, name="w2_raw")
-        w3_raw = sb.tile([P, PACK, M], F32, name="w3_raw")
+        env = sb.tile([P, T], F32, name="env")
+        w_raw = [sb.tile([P, PACK, M], F32, name=f"w_raw{i}", tag=f"w_raw{i}") for i in range(3)]
+        ramp = sb.tile([P, P], F32, name="ramp", tag="ramp", align_bytes=64)
+        ident = sb.tile([P, P], F32, name="ident")
 
         nc.vector.memset(scales[:].bitcast(I32), 0)
+        nc.gpsimd.iota(ramp[:], [[1, P]], base=0, channel_multiplier=-1, allow_small_or_imprecise_dtypes=True)
+        nc.vector.tensor_scalar(ident[:], ramp[:], 0.0, None, ALU.is_equal)
+        nc.vector.memset(env[0:ENV_ROW, :], 0.0)
 
+        nc.sync.dma_start(offs_t[:], offs)
+        nc.sync.dma_start(env[ENV_ROW:P, :], envl[0:1, :])
         nc.sync.dma_start(lag_t[:], lag)
         for q in range(4):
             nc.sync.dma_start(scales[32 * q : 32 * q + 4, :].bitcast(I32), x_scales[0, 4 * q : 4 * q + 4, :].bitcast(I32))
-        nc.sync.dma_start(offs_t[:], offs)
         nc.sync.dma_start(words[:], x_words[0].rearrange("p n t -> p (n t)").bitcast(I32))
-        nc.sync.dma_start(w3_raw[:], w3.rearrange("(p j) m -> p j m", j=PACK))
-        nc.sync.dma_start(w2_raw[:], w2.rearrange("(p j) m -> p j m", j=PACK))
-        nc.sync.dma_start(env[:], envl)
-        nc.sync.dma_start(w1_raw[:], w1.rearrange("(p j) m -> p j m", j=PACK))
+        for i in (1, 2, 0):
+            nc.sync.dma_start(w_raw[i][:], (w1, w2, w3)[i].rearrange("(p j) m -> p j m", j=PACK))
 
-        def gather(window, offsets, dtype, name, tag):
-            picked = sb.tile([P, S], dtype, name=name, tag=tag, align_bytes=64)
+        def half_of(list_tile, h):
+            return list_tile[:, h * (HALF // 16) : (h + 1) * (HALF // 16)]
+
+        def gather(window, offsets, width, dtype, name, tag):
+            picked = sb.tile([P, width], dtype, name=name, tag=tag, align_bytes=64)
             nc.vector.tensor_copy(picked[:], window.indirect(offsets))
             return picked
 
-        def quantize(raw, name):
-            grouped = sb.tile([P, M, PACK], BF16, name=name + "_grouped", tag=name + "_grouped", align_bytes=64)
-            nc.scalar.activation(
-                grouped[:].rearrange("p (c i) j -> p c j i", i=4), raw[:].rearrange("p j (c i) -> p c j i", i=4), ACT.Copy
+        def turn(picked_env, name):
+            bank = ps.tile([P, BLOCKS, P], F32, name=name, tag=name)
+            for b in range(BLOCKS):
+                nc.tensor.transpose(bank[:, b, :], picked_env[:, P * b : P * (b + 1)], ident[:])
+            return bank
+
+        def product(bank, stationary, stationary_scale, moving, moving_scale):
+            nc.tensor.matmul_mx(
+                out=bank, lhsT=stationary.bitcast(FP8X4), lhsT_scale=stationary_scale,
+                rhs=moving.bitcast(FP8X4), rhs_scale=moving_scale, start=True, stop=True,
             )
-            codes = sb.tile([P, M], U32, name=name + "_codes", align_bytes=64)
-            plane = sb.tile([P, M], U8, name=name + "_plane", align_bytes=64)
+
+        def quantize(i):
+            grouped = sb.tile([P, M, PACK], BF16, name=f"w_grouped{i}", tag=f"w_grouped{i}", align_bytes=64)
+            nc.scalar.activation(
+                grouped[:].rearrange("p (c i) j -> p c j i", i=4), w_raw[i][:].rearrange("p j (c i) -> p c j i", i=4), ACT.Copy
+            )
+            codes = sb.tile([P, M], U32, name=f"w_codes{i}", align_bytes=64)
+            plane = sb.tile([P, M], U8, name=f"w_plane{i}", align_bytes=64)
             nc.vector.quantize_mx(out=codes[:].bitcast(FP8X4), scales=plane[:], in_=grouped[:].rearrange("p m j -> p (m j)"))
             return codes, plane
 
-        def product(weights, x_codes, x_plane, name):
-            bank = ps.tile([M, S], F32, name=name)
-            nc.tensor.matmul_mx(
-                out=bank[:], lhsT=weights[0][:].bitcast(FP8X4), lhsT_scale=weights[1][:],
-                rhs=x_codes[:].bitcast(FP8X4), rhs_scale=x_plane[:], start=True, stop=True,
-            )
-            return bank
+        env_o = gather(env[:], offs_t[:], S, F32, "env_o", "ramp")
+        env_l = gather(env[:], lag_t[:], S, F32, "env_l", "env_l")
+        xo_s = gather(scales[:], offs_t[:], S, U8, "xo_s", "xo_s")
+        xo_w = gather(words[:].bitcast(U32), offs_t[:], S, U32, "xo_w", "xo_w")
+        w2_c, w2_s = quantize(1)
 
-        xl_plane = gather(scales[:], lag_t[:], U8, "xl_plane", "xl_plane")
-        xo_plane = gather(scales[:], offs_t[:], U8, "xo_plane", "xo_plane")
-        xl_codes = gather(words[:].bitcast(U32), lag_t[:], U32, "xl_codes", "xl_codes")
-        w3_q = quantize(w3_raw, "w3")
-        w2_q = quantize(w2_raw, "w2")
-        xo_codes = gather(words[:].bitcast(U32), offs_t[:], U32, "xo_codes", "w2_grouped")
+        eo_bank = turn(env_o, "eo_bank")
+        el_bank = turn(env_l, "el_bank")
+        sq = sb.tile([P, BLOCKS], F32, name="sq", tag="w_raw1")
+        nc.scalar.activation(sq[:], eo_bank[:, :, ENV_ROW], ACT.Square)
 
-        y2_bank = product(w3_q, xl_codes, xl_plane, "y2_bank")
-        y1_bank = product(w2_q, xo_codes, xo_plane, "y1_bank")
-        y2 = sb.tile([M, S], F32, name="y2")
-        nc.scalar.copy(y2[:], y2_bank[:])
+        xl_s = gather(scales[:], lag_t[:], S, U8, "xl_s", "w_grouped1")
+        w3_c, w3_s = quantize(2)
+        w1_c, w1_s = quantize(0)
+        xl_w = sb.tile([P, S], U32, name="xl_w", tag="w_grouped0", align_bytes=64)
+        for h in range(2):
+            nc.vector.tensor_copy(xl_w[:, HALF * h : HALF * (h + 1)], words[:].bitcast(U32).indirect(half_of(lag_t, h)))
 
-        env_o = gather(env[:], offs_t[:], F32, "env_o", "env_o")
-        lag_term = sb.tile([M, S], F32, name="lag_term")
-        nc.vector.tensor_tensor(lag_term[:], env[:].indirect(lag_t[:]), y2[:], ALU.mult)
-        power = sb.tile([P, S], F32, name="power")
-        nc.scalar.activation(power[:], env_o[:], ACT.Square)
-        mixed = sb.tile([M, S], F32, name="mixed", tag="env")
-        nc.vector.scalar_tensor_tensor(mixed[:], y2[:], 0.5, y1_bank[:], ALU.mult, ALU.add)
+        factors = sb.tile([P, 2, BLOCKS], F32, name="factors", tag="w_raw0")
+        half_sq, cf = factors[:, 0, :], factors[:, 1, :]
+        nc.scalar.activation(half_sq, sq[:], ACT.Copy, scale=0.5)
+        for b in range(BLOCKS):
+            nc.scalar.activation(cf[:, b : b + 1], el_bank[:, b, ENV_ROW:P], ACT.Identity, bias=half_sq[:, b : b + 1])
 
-        w1_q = quantize(w1_raw, "w1")
-        y0_bank = product(w1_q, xo_codes, xo_plane, "y0_bank")
-        power_term = sb.tile([M, S], F32, name="power_term", tag="w1_grouped", align_bytes=64)
-        nc.vector.tensor_tensor(power_term[:], power[:], mixed[:], ALU.mult)
+        def block_banks(name):
+            first = ps.tile([P, 2, M], F32, name=name + "_first", tag="first")
+            third = ps.tile([P, M], F32, name=name + "_third", tag="third")
+            fourth = ps.tile([P, M], F32, name=name + "_fourth", tag="fourth")
+            return [first[:, 0, :], first[:, 1, :], third[:], fourth[:]]
 
-        halves = [slice(HALF * h, HALF * (h + 1)) for h in range(2)]
-        both = sb.tile([M, S], F32, name="both")
-        res = sb.tile([M, S], F32, name="res")
-        for cols in halves:
-            nc.vector.tensor_tensor(both[:, cols], power_term[:, cols], lag_term[:, cols], ALU.add)
-        for cols in halves:
-            nc.vector.tensor_tensor(res[:, cols], y0_bank[:, cols], both[:, cols], ALU.add)
-            nc.sync.dma_start(out[:, cols], res[:, cols])
+        def turn_back(b, term, start, stop):
+            h, i = divmod(b, 2)
+            nc.tensor.matmul(sums[h][:, P * i : P * (i + 1)], term, ident[:], start=start, stop=stop, is_transpose=True)
+
+        sums = [ps.tile([M, HALF], F32, name=f"sums{h}") for h in range(2)]
+        y1_blocks = block_banks("y1")
+        for b in range(BLOCKS):
+            cols = slice(P * b, P * (b + 1))
+            product(y1_blocks[b], xo_w[:, cols], xo_s[:, cols], w2_c[:], w2_s[:])
+        t1 = sb.tile([P, BLOCKS, M], F32, name="t1")
+        for b in range(BLOCKS):
+            nc.scalar.activation(t1[:, b, :], y1_blocks[b], ACT.Copy, scale=sq[:, b : b + 1])
+            turn_back(b, t1[:, b, :], b % 2 == 0, False)
+        y0_bank = ps.tile([M, S], F32, name="y0_bank")
+        product(y0_bank[:], w1_c[:], w1_s[:], xo_w[:], xo_s[:])
+        y0 = sb.tile([M, S], F32, name="y0")
+        nc.scalar.copy(y0[:], y0_bank[:])
+
+        y2_blocks = block_banks("y2")
+        for b in range(BLOCKS):
+            cols = slice(P * b, P * (b + 1))
+            product(y2_blocks[b], xl_w[:, cols], xl_s[:, cols], w3_c[:], w3_s[:])
+        t2 = [sb.tile([P, M], F32, name=f"t2_{b}") for b in range(BLOCKS)]
+        for b in range(BLOCKS - 1):
+            nc.scalar.activation(t2[b][:], y2_blocks[b], ACT.Copy, scale=cf[:, b : b + 1])
+        nc.vector.tensor_scalar(t2[BLOCKS - 1][:], y2_blocks[BLOCKS - 1], cf[:, BLOCKS - 1 : BLOCKS], None, ALU.mult)
+        for h in range(2):
+            for i in range(2):
+                turn_back(2 * h + i, t2[2 * h + i][:], False, i == 1)
+            cols = slice(HALF * h, HALF * (h + 1))
+            res = sb.tile([M, HALF], F32, name=f"res{h}")
+            nc.vector.tensor_tensor(res[:], sums[h][:], y0[:, cols], ALU.add)
+            nc.sync.dma_start(out[:, cols], res[:])

from contextlib import ExitStack

import concourse.mybir as mybir

K, T, S, M = 512, 2048, 512, 128
FLOPS = 3 * 2 * K * M * S
BYTES = K * T + (K // 32) * T + 3 * K * M * 4 + T * 4 + 2 * 128 * (S // 16) * 2 + M * S * 4

F32 = mybir.dt.float32
BF16 = mybir.dt.bfloat16
I32 = mybir.dt.int32
U32 = mybir.dt.uint32
U16 = mybir.dt.uint16
U8 = mybir.dt.uint8
FP8X4 = mybir.dt.float8_e4m3fn_x4
ACT = mybir.ActivationFunctionType
ALU = mybir.AluOpType

P = 128
PACK = 4
HALF = S // 2
BLOCKS = S // P
ENV_ROW = P - 1


def tile_picked_ymempol_lin_p_kernel(tc, x_words, x_scales, w1, w2, w3, envl, offs, lag, out):
    nc = tc.nc
    with ExitStack() as ctx:
        sb = ctx.enter_context(tc.tile_pool(name="sb", bufs=1))
        ps = ctx.enter_context(tc.psum_pool(name="ps", bufs=1))

        offs_t = sb.tile([P, S // 16], U16, name="offs_t")
        lag_t = sb.tile([P, S // 16], U16, name="lag_t")
        words = sb.tile([P, T], I32, name="words")
        scales = sb.tile([P, T], U8, name="scales")
        env = sb.tile([P, T], F32, name="env")
        w_raw = [sb.tile([P, PACK, M], F32, name=f"w_raw{i}", tag=f"w_raw{i}") for i in range(3)]
        ramp = sb.tile([P, P], F32, name="ramp", tag="ramp", align_bytes=64)
        ident = sb.tile([P, P], F32, name="ident")

        nc.vector.memset(scales[:].bitcast(I32), 0)
        nc.gpsimd.iota(ramp[:], [[1, P]], base=0, channel_multiplier=-1, allow_small_or_imprecise_dtypes=True)
        nc.vector.tensor_scalar(ident[:], ramp[:], 0.0, None, ALU.is_equal)
        nc.vector.memset(env[0:ENV_ROW, :], 0.0)

        nc.sync.dma_start(offs_t[:], offs)
        nc.sync.dma_start(env[ENV_ROW:P, :], envl[0:1, :])
        nc.sync.dma_start(lag_t[:], lag)
        for q in range(4):
            nc.sync.dma_start(scales[32 * q : 32 * q + 4, :].bitcast(I32), x_scales[0, 4 * q : 4 * q + 4, :].bitcast(I32))
        nc.sync.dma_start(words[:], x_words[0].rearrange("p n t -> p (n t)").bitcast(I32))
        for i in (1, 2, 0):
            nc.sync.dma_start(w_raw[i][:], (w1, w2, w3)[i].rearrange("(p j) m -> p j m", j=PACK))

        def half_of(list_tile, h):
            return list_tile[:, h * (HALF // 16) : (h + 1) * (HALF // 16)]

        def gather(window, offsets, width, dtype, name, tag):
            picked = sb.tile([P, width], dtype, name=name, tag=tag, align_bytes=64)
            nc.vector.tensor_copy(picked[:], window.indirect(offsets))
            return picked

        def turn(picked_env, name):
            bank = ps.tile([P, BLOCKS, P], F32, name=name, tag=name)
            for b in range(BLOCKS):
                nc.tensor.transpose(bank[:, b, :], picked_env[:, P * b : P * (b + 1)], ident[:])
            return bank

        def product(bank, stationary, stationary_scale, moving, moving_scale):
            nc.tensor.matmul_mx(
                out=bank, lhsT=stationary.bitcast(FP8X4), lhsT_scale=stationary_scale,
                rhs=moving.bitcast(FP8X4), rhs_scale=moving_scale, start=True, stop=True,
            )

        def quantize(i):
            grouped = sb.tile([P, M, PACK], BF16, name=f"w_grouped{i}", tag=f"w_grouped{i}", align_bytes=64)
            nc.scalar.activation(
                grouped[:].rearrange("p (c i) j -> p c j i", i=4), w_raw[i][:].rearrange("p j (c i) -> p c j i", i=4), ACT.Copy
            )
            codes = sb.tile([P, M], U32, name=f"w_codes{i}", align_bytes=64)
            plane = sb.tile([P, M], U8, name=f"w_plane{i}", align_bytes=64)
            nc.vector.quantize_mx(out=codes[:].bitcast(FP8X4), scales=plane[:], in_=grouped[:].rearrange("p m j -> p (m j)"))
            return codes, plane

        env_o = gather(env[:], offs_t[:], S, F32, "env_o", "ramp")
        env_l = gather(env[:], lag_t[:], S, F32, "env_l", "env_l")
        xo_s = gather(scales[:], offs_t[:], S, U8, "xo_s", "xo_s")
        xo_w = gather(words[:].bitcast(U32), offs_t[:], S, U32, "xo_w", "xo_w")
        w2_c, w2_s = quantize(1)

        eo_bank = turn(env_o, "eo_bank")
        el_bank = turn(env_l, "el_bank")
        sq = sb.tile([P, BLOCKS], F32, name="sq", tag="w_raw1")
        nc.scalar.activation(sq[:], eo_bank[:, :, ENV_ROW], ACT.Square)

        xl_s = gather(scales[:], lag_t[:], S, U8, "xl_s", "w_grouped1")
        w3_c, w3_s = quantize(2)
        w1_c, w1_s = quantize(0)
        xl_w = sb.tile([P, S], U32, name="xl_w", tag="w_grouped0", align_bytes=64)
        for h in range(2):
            nc.vector.tensor_copy(xl_w[:, HALF * h : HALF * (h + 1)], words[:].bitcast(U32).indirect(half_of(lag_t, h)))

        factors = sb.tile([P, 2, BLOCKS], F32, name="factors", tag="w_raw0")
        half_sq, cf = factors[:, 0, :], factors[:, 1, :]
        nc.scalar.activation(half_sq, sq[:], ACT.Copy, scale=0.5)
        for b in range(BLOCKS):
            nc.scalar.activation(cf[:, b : b + 1], el_bank[:, b, ENV_ROW:P], ACT.Identity, bias=half_sq[:, b : b + 1])

        def block_banks(name):
            first = ps.tile([P, 2, M], F32, name=name + "_first", tag="first")
            third = ps.tile([P, M], F32, name=name + "_third", tag="third")
            fourth = ps.tile([P, M], F32, name=name + "_fourth", tag="fourth")
            return [first[:, 0, :], first[:, 1, :], third[:], fourth[:]]

        def turn_back(b, term, start, stop):
            h, i = divmod(b, 2)
            nc.tensor.matmul(sums[h][:, P * i : P * (i + 1)], term, ident[:], start=start, stop=stop, is_transpose=True)

        sums = [ps.tile([M, HALF], F32, name=f"sums{h}") for h in range(2)]
        y1_blocks = block_banks("y1")
        for b in range(BLOCKS):
            cols = slice(P * b, P * (b + 1))
            product(y1_blocks[b], xo_w[:, cols], xo_s[:, cols], w2_c[:], w2_s[:])
        t1 = sb.tile([P, BLOCKS, M], F32, name="t1")
        for b in range(BLOCKS):
            nc.scalar.activation(t1[:, b, :], y1_blocks[b], ACT.Copy, scale=sq[:, b : b + 1])
            turn_back(b, t1[:, b, :], b % 2 == 0, False)
        y0_bank = ps.tile([M, S], F32, name="y0_bank")
        product(y0_bank[:], w1_c[:], w1_s[:], xo_w[:], xo_s[:])
        y0 = sb.tile([M, S], F32, name="y0")
        nc.scalar.copy(y0[:], y0_bank[:])

        y2_blocks = block_banks("y2")
        for b in range(BLOCKS):
            cols = slice(P * b, P * (b + 1))
            product(y2_blocks[b], xl_w[:, cols], xl_s[:, cols], w3_c[:], w3_s[:])
        t2 = [sb.tile([P, M], F32, name=f"t2_{b}") for b in range(BLOCKS)]
        for b in range(BLOCKS - 1):
            nc.scalar.activation(t2[b][:], y2_blocks[b], ACT.Copy, scale=cf[:, b : b + 1])
        nc.vector.tensor_scalar(t2[BLOCKS - 1][:], y2_blocks[BLOCKS - 1], cf[:, BLOCKS - 1 : BLOCKS], None, ALU.mult)
        for h in range(2):
            for i in range(2):
                turn_back(2 * h + i, t2[2 * h + i][:], False, i == 1)
            cols = slice(HALF * h, HALF * (h + 1))
            res = sb.tile([M, HALF], F32, name=f"res{h}")
            nc.vector.tensor_tensor(res[:], sums[h][:], y0[:, cols], ALU.add)
            nc.sync.dma_start(out[:, cols], res[:])
